import numpy as np
import ml_dtypes


def mxq(x, axis, fmt="e4m3"):
    dtype, down = {"e4m3": (ml_dtypes.float8_e4m3fn, 7), "e5m2": (ml_dtypes.float8_e5m2, 14)}[fmt]
    v = np.moveaxis(np.asarray(x, np.float32).astype(ml_dtypes.bfloat16).astype(np.float64), axis, -1)
    blocks = v.reshape(v.shape[:-1] + (-1, 32))
    amax = np.abs(blocks).max(-1, keepdims=True)
    byte = np.maximum(np.where(amax > 0, np.frexp(amax)[1] - 1 + 127, 0) - down, 1)
    scale = np.exp2(byte - 127.0)
    codes = (blocks / scale).astype(np.float32).astype(dtype).astype(np.float64)
    return np.moveaxis((codes * scale).reshape(v.shape), -1, axis)


WIDE = False


def mx_kscale(k):
    if not WIDE:
        return np.ones(k)
    levels = np.array([10, -10, 5, -5, 0])
    if k % 512:
        return np.exp2(np.random.permutation(np.resize(levels, k // 32))).repeat(32)
    a = np.empty((k // 512, 16))
    for p in range(k // 512):
        a[p, :8] = np.random.permutation(np.resize(levels, 8))
        for g in range(8):
            far = levels[np.abs(levels - a[p, g]) >= 10]
            a[p, g + 8] = far[np.random.randint(len(far))]
    return np.exp2(a.ravel()).repeat(32)


def f64(x):
    return np.asarray(x).astype(np.float64)


def striped(idx):
    return np.tile(np.asarray(idx).reshape(-1, 16).T, (8, 1)).astype(np.uint16)


def unstriped(offs):
    return offs[:16].T.reshape(-1).astype(np.int64)


def striped8(idx):
    return np.asarray(idx).reshape(8, -1, 16).transpose(0, 2, 1).reshape(128, -1).astype(np.uint16)


def unstriped8(offs):
    return offs.reshape(8, 16, -1).transpose(0, 2, 1).reshape(8, -1).astype(np.int64)


def pick8(x, idx, run):
    r = np.arange(len(x))
    return x[r[:, None], idx[r % (8 * run) // run]]


E2M1 = np.array([0.0, 0.5, 1.0, 1.5, 2.0, 3.0, 4.0, 6.0, -0.0, -0.5, -1.0, -1.5, -2.0, -3.0, -4.0, -6.0])


def pack_weight(w, fmt):
    k, n = w.shape
    w = f64(np.asarray(w, np.float32).astype(ml_dtypes.bfloat16)).reshape(k // 32, 32, n)
    amax = np.abs(w).max(1)
    if fmt == "e4m3":
        byte = np.frexp(amax)[1] - 1 + 127 - 7
    else:
        mant, ex = np.frexp(amax / 6.0)
        byte = np.where(mant > 0.5, ex, ex - 1) + 127
    byte = np.clip(np.where(amax > 0, byte, 1), 1, 254)
    scaled = (w * np.exp2(127.0 - byte)[:, None, :]).reshape(k, n).astype(np.float32)
    by_word = np.ascontiguousarray(scaled.reshape(k // 512, 128, 4, n).transpose(0, 1, 3, 2))
    if fmt == "e4m3":
        words = by_word.astype(ml_dtypes.float8_e4m3fn).view(np.uint8)
    else:
        c = by_word.astype(ml_dtypes.float4_e2m1fn).view(np.uint8) & 0xF
        words = (c[..., 0::2] | (c[..., 1::2] << 4)).reshape(k // 512, 128, 2 * n)
    return np.ascontiguousarray(words), np.ascontiguousarray(byte.astype(np.uint8).reshape(k // 512, 16, n))


def unpack_weight(words, scales, fmt):
    g, _, n = scales.shape
    words = np.ascontiguousarray(words).reshape(g, 128, n, -1)
    if fmt == "e4m3":
        vals = words.view(ml_dtypes.float8_e4m3fn).astype(np.float64)
    else:
        nib = np.empty((g, 128, n, 4), np.uint8)
        nib[..., 0::2] = words & 0xF
        nib[..., 1::2] = words >> 4
        vals = E2M1[nib]
    vals = vals * np.repeat(np.exp2(scales.astype(np.float64) - 127.0), 8, axis=1)[..., None]
    return vals.transpose(0, 1, 3, 2).reshape(g * 512, n)


K, J, R, T, Z, M, C, N, U = 512, 256, 512, 1024, 512, 1024, 512, 256, 1024


def setup_inputs():
    n = np.random.standard_normal
    idx = np.random.permutation(T)[:J]
    idx2 = np.random.permutation(M)[:J]
    idx3 = np.stack([np.random.permutation(C)[:J] for _ in range(8)])
    idx4 = np.stack([np.random.permutation(C)[:J] for _ in range(8)])
    idx5 = np.stack([np.random.permutation(U)[:C] for _ in range(8)])
    fk = mx_kscale(K)
    fr = mx_kscale(R)
    fz = mx_kscale(Z)
    xtp = pack_weight(n((K, T)) * fk[:, None], "e4m3")
    wp = pack_weight(n((K, R)) * 1 / np.sqrt(K) / fk[:, None] * fr, "e4m3")
    xop = pack_weight(n((Z, M)) / fz[:, None], "e4m3")
    w2p = pack_weight(n((Z, R)) * 1 / np.sqrt(Z) * fz[:, None] * fr, "e2m1")
    wbp = pack_weight(n((R, N)) * 1 / np.sqrt(R) / fr[:, None], "e2m1")
    return {
        "xt_words": xtp[0],
        "xt_scales": xtp[1],
        "w_words": wp[0],
        "w_scales": wp[1],
        "xo_words": xop[0],
        "xo_scales": xop[1],
        "w2_words": w2p[0],
        "w2_scales": w2p[1],
        "wb_words": wbp[0],
        "wb_scales": wbp[1],
        "offs": striped(idx),
        "offs2": striped(idx2),
        "offs3": striped8(idx3),
        "offs4": striped8(idx4),
        "offs5": striped8(idx5),
    }


def reference(xt_words, xt_scales, w_words, w_scales, xo_words, xo_scales, w2_words, w2_scales, wb_words, wb_scales, offs, offs2, offs3, offs4, offs5):
    idx = unstriped(offs)
    idx2 = unstriped(offs2)
    idx3 = unstriped8(offs3)
    idx4 = unstriped8(offs4)
    idx5 = unstriped8(offs5)
    xtu = unpack_weight(xt_words, xt_scales, "e4m3")
    wu = unpack_weight(w_words, w_scales, "e4m3")
    xou = unpack_weight(xo_words, xo_scales, "e4m3")
    w2u = unpack_weight(w2_words, w2_scales, "e2m1")
    wbu = unpack_weight(wb_words, wb_scales, "e2m1")
    xtidxg = xtu[:, idx]
    a = wu.T @ xtidxg
    xoidx2g = xou[:, idx2]
    b = w2u.T @ xoidx2g
    pw = np.zeros((R, C))
    pw[np.arange(R)[:, None], idx3[np.arange(R) % 512 // 64]] = a
    pv = np.zeros((R, C))
    pv[np.arange(R)[:, None], idx4[np.arange(R) % 512 // 64]] = b
    g0 = np.pad(pw, ((0, 0), (1, 0)))[:, :C]
    g1 = pw + g0
    g2 = np.pad(g1, ((0, 0), (2, 0)))[:, :C]
    g3 = g1 + g2
    hid = np.maximum(g3, pv)
    hidq = mxq(hid, 0, "e4m3")
    p = wbu.T @ hidq
    m0 = np.zeros((N, U))
    m0[np.arange(N)[:, None], idx5[np.arange(N) % 128 // 16]] = p
    m1 = np.pad(m0, ((0, 0), (1, 0)))[:, :U]
    y = m0 - m1
    return y

@@ -1,0 +1,209 @@
+from contextlib import ExitStack
+
+import concourse.mybir as mybir
+
+K, J, R, T, Z, M, C, N, U = 512, 256, 512, 1024, 512, 1024, 512, 256, 1024
+FLOPS = 2 * (K * R * J + Z * R * J + R * N * C)
+
+P = 128
+PACK = 4
+F32 = mybir.dt.float32
+BF16 = mybir.dt.bfloat16
+I32 = mybir.dt.int32
+U32 = mybir.dt.uint32
+U16 = mybir.dt.uint16
+U8 = mybir.dt.uint8
+FP8X4 = mybir.dt.float8_e4m3fn_x4
+FP4X4 = mybir.dt.float4_e2m1fn_x4
+ADD = mybir.AluOpType.add
+SUB = mybir.AluOpType.subtract
+MAX = mybir.AluOpType.max
+COPY = mybir.ActivationFunctionType.Copy
+
+CHUNKS = ((0, 128), (128, 256), (256, 512))
+STORE_COLS = 256
+
+
+def tile_picked_tokens_plain_two_trailing_one_endsteps_kernel(
+    tc, xt_words, xt_scales, w_words, w_scales, xo_words, xo_scales, w2_words, w2_scales,
+    wb_words, wb_scales, offs, offs2, offs3, offs4, offs5, out,
+):
+    nc = tc.nc
+    with ExitStack() as ctx:
+        lists = ctx.enter_context(tc.tile_pool(name="lists", bufs=1))
+        keep = ctx.enter_context(tc.tile_pool(name="keep", bufs=1))
+        reuse = ctx.enter_context(tc.tile_pool(name="reuse", bufs=1))
+        psum = ctx.enter_context(tc.psum_pool(name="psum", bufs=8))
+
+        def load_list(name, src):
+            tile = lists.tile(list(src.shape), U16, name=name)
+            nc.sync.dma_start(tile[:], src)
+            return tile
+
+        def zeroed_plane(name, width, engine):
+            plane = keep.tile([P, width], U8, name=name, align_bytes=64)
+            engine.memset(plane[:].bitcast(I32), 0)
+            return plane
+
+        def load_scales(plane, src):
+            rows = src[0].bitcast(I32)
+            for q in range(4):
+                nc.sync.dma_start(plane[32 * q : 32 * q + 4, :].bitcast(I32), rows[4 * q : 4 * q + 4, :])
+
+        def e4m3_words(src):
+            return src[0].rearrange("p c r -> p (c r)").bitcast(I32)
+
+        xts_win = zeroed_plane("xts_win", T, nc.vector)
+        ws_raw = zeroed_plane("ws_raw", R, nc.vector)
+        idx = load_list("idx", offs)
+        w_stage = keep.tile([4, 4, R // 4], I32, name="w_stage")
+        nc.sync.dma_start(w_stage[:], w_scales[0].bitcast(I32).rearrange("(q i) n -> i q n", i=4))
+        load_scales(xts_win, xt_scales)
+        xt_win = keep.tile([P, T], U32, name="xt_win")
+        nc.sync.dma_start(xt_win[:].bitcast(I32), e4m3_words(xt_words))
+        w_raw = reuse.tile([P, R], U32, name="w_raw", offset=0)
+        nc.sync.dma_start(w_raw[:].bitcast(I32), e4m3_words(w_words))
+        idx3 = load_list("idx3", offs3)
+
+        xos_win = zeroed_plane("xos_win", M, nc.gpsimd)
+        w2s_raw = zeroed_plane("w2s_raw", R, nc.gpsimd)
+        wbs = zeroed_plane("wbs", N, nc.gpsimd)
+
+        idx2 = load_list("idx2", offs2)
+        load_scales(xos_win, xo_scales)
+        xo_win = keep.tile([P, M], U32, name="xo_win")
+        nc.sync.dma_start(xo_win[:].bitcast(I32), e4m3_words(xo_words))
+        w2_raw = keep.tile([P, 2 * R], U8, name="w2_raw")
+        nc.sync.dma_start(w2_raw[:].bitcast(I32), w2_words[0].bitcast(I32))
+        load_scales(w2s_raw, w2_scales)
+        idx4 = load_list("idx4", offs4)
+        idx5 = load_list("idx5", offs5)
+        wb = keep.tile([P, 2 * N], U8, name="wb", align_bytes=64)
+        nc.sync.dma_start(wb[:].bitcast(I32), wb_words[0].bitcast(I32))
+        load_scales(wbs, wb_scales)
+
+        pw = []
+        for t in range(PACK):
+            board = reuse.tile([P, C], F32, name="pw%d" % t, offset=16384 + 2048 * t)
+            nc.gpsimd.memset(board[:], 0.0)
+            pw.append(board)
+
+        xts = keep.tile([P, J], U8, name="xts", align_bytes=64)
+        nc.vector.tensor_copy(xts[:], xts_win[:].indirect(idx[:]))
+        for q in range(4):
+            nc.vector.tensor_copy(ws_raw[32 * q : 32 * q + 4, :].bitcast(I32), w_stage[:, q, :])
+        ws = keep.tile([P, PACK, P], U8, name="ws", align_bytes=64)
+        nc.vector.tensor_copy(ws[:], ws_raw[:].rearrange("p (m t) -> p t m", t=PACK))
+        xt = keep.tile([P, J], U32, name="xt", align_bytes=64)
+        nc.vector.tensor_copy(xt[:], xt_win[:].indirect(idx[:]))
+        w_first = reuse.tile([P, P], U32, name="w_first", align_bytes=64, offset=2048)
+        w_rest = reuse.tile([P, PACK - 1, P], U32, name="w_rest", align_bytes=64, offset=2048 + 512)
+        w_by_t = w_raw[:].rearrange("p (m t) -> p t m", t=PACK)
+        nc.scalar.copy(w_first[:], w_by_t[:, 0, :])
+        nc.scalar.copy(w_rest[:], w_by_t[:, 1:, :])
+
+        a_vals = []
+        for t in range(PACK):
+            acc = psum.tile([P, J], F32, name="acc")
+            lhs = w_first[:] if t == 0 else w_rest[:, t - 1, :]
+            nc.tensor.matmul_mx(acc[:], lhsT=lhs.bitcast(FP8X4), lhsT_scale=ws[:, t, :],
+                                rhs=xt[:].bitcast(FP8X4), rhs_scale=xts[:], start=True, stop=True)
+            vals = reuse.tile([P, J], F32, name="a%d" % t, offset=4096 + 1024 * t)
+            if t == 0:
+                nc.scalar.activation(vals[:], acc[:], COPY)
+            else:
+                nc.vector.tensor_copy(vals[:], acc[:])
+            nc.scalar.activation(pw[t][:].indirect(idx3[:]), vals[:], COPY)
+            a_vals.append(vals)
+
+        pv = []
+        for t in range(PACK):
+            board = reuse.tile([P, C], F32, name="pv%d" % t, offset=2048 * t)
+            nc.gpsimd.memset(board[:], 0.0)
+            pv.append(board)
+        xos = keep.tile([P, J], U8, name="xos", align_bytes=64)
+        nc.vector.tensor_copy(xos[:], xos_win[:].indirect(idx2[:]))
+        xo = reuse.tile([P, J], U32, name="xo", align_bytes=64, offset=8192)
+        nc.vector.tensor_copy(xo[:], xo_win[:].indirect(idx2[:]))
+        w2s = keep.tile([P, PACK, P], U8, name="w2s", align_bytes=64)
+        nc.vector.tensor_copy(w2s[:], w2s_raw[:].rearrange("p (m t) -> p t m", t=PACK))
+        w2 = reuse.tile([P, PACK, 2 * P], U8, name="w2", align_bytes=64, offset=24576)
+        nc.vector.tensor_copy(w2[:].rearrange("p t (m e) -> p t m e", e=2),
+                              w2_raw[:].rearrange("p (m t e) -> p t m e", t=PACK, e=2))
+        b_vals = []
+        for pair in range(PACK // 2):
+            acc = psum.tile([P, 2, J], F32, name="acc")
+            for e in range(2):
+                t = 2 * pair + e
+                nc.tensor.matmul_mx(acc[:, e, :], lhsT=w2[:, t, :].bitcast(FP4X4), lhsT_scale=w2s[:, t, :],
+                                    rhs=xo[:].bitcast(FP8X4), rhs_scale=xos[:], start=True, stop=True)
+            vals = keep.tile([P, 2, J], F32, name="b%d" % pair)
+            nc.vector.tensor_copy(vals[:], acc[:])
+            b_vals.append(vals)
+
+        g1_bufs = []
+        for e, offset in enumerate((24576, 8192)):
+            buf = reuse.tile([P, C + 2], F32, name="g1_%d" % e, offset=offset)
+            nc.vector.memset(buf[:, 0:2], 0.0)
+            g1_bufs.append(buf)
+        g3 = keep.tile([P, PACK, C], F32, name="g3")
+        for t in range(PACK):
+            g1 = g1_bufs[t % 2]
+            nc.vector.tensor_copy(g1[:, 2:3], pw[t][:, 0:1])
+            nc.vector.tensor_tensor(g1[:, 3:], pw[t][:, 1:], pw[t][:, : C - 1], ADD)
+            nc.vector.tensor_tensor(g3[:, t, :], g1[:, 2:], g1[:, :C], ADD)
+
+        pages = []
+        for i in range(N // P):
+            page = reuse.tile([P, U], F32, name="page%d" % i, offset=16384 + 4096 * i)
+            nc.gpsimd.memset(page[:], 0.0)
+            pages.append(page)
+
+        hid = keep.tile([P, PACK - 1, C], F32, name="hid")
+        for t in range(PACK):
+            nc.scalar.activation(pv[t][:].indirect(idx4[:]), b_vals[t // 2][:, t % 2, :], COPY)
+            if t < PACK - 1:
+                nc.vector.tensor_tensor(hid[:, t, :], g3[:, t, :], pv[t][:], MAX)
+
+        last = PACK - 1
+        woven = {}
+        for c0, c1 in CHUNKS:
+            woven[c0] = keep.tile([P, c1 - c0, PACK], BF16, name="woven%d" % c0, align_bytes=64)
+            nc.vector.tensor_copy(woven[c0][:, :, :last], hid[:, :, c0:c1].rearrange("p t c -> p c t"))
+        for c0, c1 in CHUNKS:
+            width = c1 - c0
+            nc.vector.tensor_tensor(woven[c0][:, :, last], g3[:, last, c0:c1], pv[last][:, c0:c1], MAX)
+            codes = keep.tile([P, width], U32, name="codes%d" % c0, align_bytes=64)
+            scales = keep.tile([P, width], U8, name="scales%d" % c0, align_bytes=64)
+            nc.vector.quantize_mx(codes[:].bitcast(FP8X4), scales[:], woven[c0][:].rearrange("p c t -> p (c t)"))
+            p_vals = keep.tile([P, N // P, width], F32, name="p%d" % c0)
+
+            def product(acc, i):
+                nc.tensor.matmul_mx(acc, lhsT=wb[:, 2 * P * i : 2 * P * (i + 1)].bitcast(FP4X4),
+                                    lhsT_scale=wbs[:, P * i : P * (i + 1)],
+                                    rhs=codes[:].bitcast(FP8X4), rhs_scale=scales[:], start=True, stop=True)
+
+            if c0 == 0:
+                accs = [psum.tile([P, width], F32, name="acc") for i in range(N // P)]
+                for i in range(N // P):
+                    product(accs[i][:], i)
+                nc.scalar.activation(p_vals[:, 0, :], accs[0][:], COPY)
+                nc.vector.tensor_copy(p_vals[:, 1, :], accs[1][:])
+            else:
+                acc = psum.tile([P, N // P, width], F32, name="acc")
+                for i in range(N // P):
+                    product(acc[:, i, :], i)
+                nc.vector.tensor_copy(p_vals[:], acc[:])
+            for i in range(N // P):
+                nc.scalar.activation(pages[i][:].indirect(idx5[:, c0 // 16 : c1 // 16]), p_vals[:, i, :], COPY)
+
+        for i in range(N // P):
+            y = keep.tile([P, U], F32, name="y%d" % i)
+            if i == 0:
+                nc.vector.tensor_copy(y[:, 0:1], pages[i][:, 0:1])
+            else:
+                nc.scalar.copy(y[:, 0:1], pages[i][:, 0:1])
+            for u0 in range(0, U, STORE_COLS):
+                lo, hi = max(u0, 1), u0 + STORE_COLS
+                nc.vector.tensor_tensor(y[:, lo:hi], pages[i][:, lo:hi], pages[i][:, lo - 1 : hi - 1], SUB)
+                nc.sync.dma_start(out[P * i : P * (i + 1), u0:hi], y[:, u0:hi])

@@ -54,82 +54,93 @@ def tile_picked_tokens_plain_two_trailing_one_endsteps_kernel(
             return src[0].rearrange("p c r -> p (c r)").bitcast(I32)
 
         xts_win = zeroed_plane("xts_win", T, nc.vector)
-        ws_raw = zeroed_plane("ws_raw", R, nc.vector)
+        ws_raw = reuse.tile([P, R], U8, name="ws_raw", offset=23552)
+        nc.vector.memset(ws_raw[:].bitcast(I32), 0)
         idx = load_list("idx", offs)
-        w_stage = keep.tile([4, 4, R // 4], I32, name="w_stage")
-        nc.sync.dma_start(w_stage[:], w_scales[0].bitcast(I32).rearrange("(q i) n -> i q n", i=4))
-        load_scales(xts_win, xt_scales)
-        xt_win = keep.tile([P, T], U32, name="xt_win")
+        xts_stage = keep.tile([P, 2, T // 4], I32, name="xts_stage")
+        xts_rows = xt_scales[0].bitcast(I32)
+        for part in range(2):
+            nc.sync.dma_start(xts_stage[64 * part : 64 * part + 4, :, :],
+                              xts_rows[8 * part : 8 * part + 8, :].rearrange("(q i) n -> i q n", i=4))
+        w2s_stage = keep.tile([4, 4, R // 4], I32, name="w2s_stage")
+        nc.sync.dma_start(w2s_stage[:], w2_scales[0].bitcast(I32).rearrange("(q i) n -> i q n", i=4))
+        xt_win = reuse.tile([P, T], U32, name="xt_win", offset=0)
         nc.sync.dma_start(xt_win[:].bitcast(I32), e4m3_words(xt_words))
-        w_raw = reuse.tile([P, R], U32, name="w_raw", offset=0)
+        w_raw = reuse.tile([P, R], U32, name="w_raw", offset=4096)
         nc.sync.dma_start(w_raw[:].bitcast(I32), e4m3_words(w_words))
         idx3 = load_list("idx3", offs3)
+        idx2 = load_list("idx2", offs2)
+        load_scales(ws_raw, w_scales)
 
         xos_win = zeroed_plane("xos_win", M, nc.gpsimd)
-        w2s_raw = zeroed_plane("w2s_raw", R, nc.gpsimd)
         wbs = zeroed_plane("wbs", N, nc.gpsimd)
 
-        idx2 = load_list("idx2", offs2)
-        load_scales(xos_win, xo_scales)
         xo_win = keep.tile([P, M], U32, name="xo_win")
         nc.sync.dma_start(xo_win[:].bitcast(I32), e4m3_words(xo_words))
         w2_raw = keep.tile([P, 2 * R], U8, name="w2_raw")
         nc.sync.dma_start(w2_raw[:].bitcast(I32), w2_words[0].bitcast(I32))
-        load_scales(w2s_raw, w2_scales)
+        load_scales(xos_win, xo_scales)
         idx4 = load_list("idx4", offs4)
-        idx5 = load_list("idx5", offs5)
         wb = keep.tile([P, 2 * N], U8, name="wb", align_bytes=64)
         nc.sync.dma_start(wb[:].bitcast(I32), wb_words[0].bitcast(I32))
+        idx5 = load_list("idx5", offs5)
         load_scales(wbs, wb_scales)
 
         pw = []
         for t in range(PACK):
-            board = reuse.tile([P, C], F32, name="pw%d" % t, offset=16384 + 2048 * t)
+            board = reuse.tile([P, C], F32, name="pw%d" % t, offset=15360 + 2048 * t)
             nc.gpsimd.memset(board[:], 0.0)
             pw.append(board)
 
-        xts = keep.tile([P, J], U8, name="xts", align_bytes=64)
-        nc.vector.tensor_copy(xts[:], xts_win[:].indirect(idx[:]))
         for q in range(4):
-            nc.vector.tensor_copy(ws_raw[32 * q : 32 * q + 4, :].bitcast(I32), w_stage[:, q, :])
-        ws = keep.tile([P, PACK, P], U8, name="ws", align_bytes=64)
-        nc.vector.tensor_copy(ws[:], ws_raw[:].rearrange("p (m t) -> p t m", t=PACK))
-        xt = keep.tile([P, J], U32, name="xt", align_bytes=64)
+            base = 64 * (q // 2)
+            nc.vector.tensor_copy(xts_win[32 * q : 32 * q + 4, :].bitcast(I32), xts_stage[base : base + 4, q % 2, :])
+        half = J // 2
+        xts = keep.tile([P, J], U8, name="xts", align_bytes=64)
+        xt = reuse.tile([P, J], U32, name="xt", align_bytes=64, offset=8704)
+        nc.vector.tensor_copy(xts[:], xts_win[:].indirect(idx[:]))
         nc.vector.tensor_copy(xt[:], xt_win[:].indirect(idx[:]))
-        w_first = reuse.tile([P, P], U32, name="w_first", align_bytes=64, offset=2048)
-        w_rest = reuse.tile([P, PACK - 1, P], U32, name="w_rest", align_bytes=64, offset=2048 + 512)
-        w_by_t = w_raw[:].rearrange("p (m t) -> p t m", t=PACK)
-        nc.scalar.copy(w_first[:], w_by_t[:, 0, :])
-        nc.scalar.copy(w_rest[:], w_by_t[:, 1:, :])
+        ws_first = reuse.tile([P, P], U8, name="ws_first", align_bytes=64, offset=0)
+        ws_rest = reuse.tile([P, PACK - 1, P], U8, name="ws_rest", align_bytes=64, offset=128)
+        ws_by_t = ws_raw[:].rearrange("p (m t) -> p t m", t=PACK)
+        nc.vector.tensor_copy(ws_first[:], ws_by_t[:, 0, :])
+        nc.vector.tensor_copy(ws_rest[:], ws_by_t[:, 1:, :])
+        w_first = reuse.tile([P, P], U32, name="w_first", align_bytes=64, offset=6144)
+        w_rest = reuse.tile([P, PACK - 1, P], U32, name="w_rest", align_bytes=64, offset=6656)
+        w_by_m = w_raw[:].rearrange("p (m t) -> p m t", t=PACK)
+        nc.scalar.copy(w_first[:], w_by_m[:, :, 0])
+        nc.scalar.copy(w_rest[:].rearrange("p t m -> p m t"), w_by_m[:, :, 1:])
 
-        a_vals = []
-        for t in range(PACK):
-            acc = psum.tile([P, J], F32, name="acc")
-            lhs = w_first[:] if t == 0 else w_rest[:, t - 1, :]
-            nc.tensor.matmul_mx(acc[:], lhsT=lhs.bitcast(FP8X4), lhsT_scale=ws[:, t, :],
-                                rhs=xt[:].bitcast(FP8X4), rhs_scale=xts[:], start=True, stop=True)
-            vals = reuse.tile([P, J], F32, name="a%d" % t, offset=4096 + 1024 * t)
-            if t == 0:
-                nc.scalar.activation(vals[:], acc[:], COPY)
+        a_vals = [reuse.tile([P, J], F32, name="a%d" % t, offset=11264 + 1024 * t) for t in range(PACK)]
+        for step, (t, j0, j1) in enumerate(((0, 0, half), (1, 0, J), (0, half, J), (2, 0, J), (3, 0, J))):
+            acc = psum.tile([P, j1 - j0], F32, name="acc")
+            w_t, ws_t = (w_first[:], ws_first[:]) if t == 0 else (w_rest[:, t - 1, :], ws_rest[:, t - 1, :])
+            nc.tensor.matmul_mx(acc[:], lhsT=w_t.bitcast(FP8X4), lhsT_scale=ws_t,
+                                rhs=xt[:, j0:j1].bitcast(FP8X4), rhs_scale=xts[:, j0:j1], start=True, stop=True)
+            if step == 0:
+                nc.scalar.activation(a_vals[t][:, j0:j1], acc[:], COPY)
             else:
-                nc.vector.tensor_copy(vals[:], acc[:])
-            nc.scalar.activation(pw[t][:].indirect(idx3[:]), vals[:], COPY)
-            a_vals.append(vals)
+                nc.vector.tensor_copy(a_vals[t][:, j0:j1], acc[:])
+            nc.scalar.activation(pw[t][:].indirect(idx3[:, j0 // 16 : j1 // 16]), a_vals[t][:, j0:j1], COPY)
 
-        pv = []
-        for t in range(PACK):
-            board = reuse.tile([P, C], F32, name="pv%d" % t, offset=2048 * t)
-            nc.gpsimd.memset(board[:], 0.0)
-            pv.append(board)
-        xos = keep.tile([P, J], U8, name="xos", align_bytes=64)
-        nc.vector.tensor_copy(xos[:], xos_win[:].indirect(idx2[:]))
-        xo = reuse.tile([P, J], U32, name="xo", align_bytes=64, offset=8192)
-        nc.vector.tensor_copy(xo[:], xo_win[:].indirect(idx2[:]))
+        w2s_raw = reuse.tile([P, R], U8, name="w2s_raw", offset=23552)
+        nc.vector.memset(w2s_raw[:].bitcast(I32), 0)
+        for q in range(4):
+            nc.vector.tensor_copy(w2s_raw[32 * q : 32 * q + 4, :].bitcast(I32), w2s_stage[:, q, :])
         w2s = keep.tile([P, PACK, P], U8, name="w2s", align_bytes=64)
         nc.vector.tensor_copy(w2s[:], w2s_raw[:].rearrange("p (m t) -> p t m", t=PACK))
-        w2 = reuse.tile([P, PACK, 2 * P], U8, name="w2", align_bytes=64, offset=24576)
+        xo = reuse.tile([P, J], U32, name="xo", align_bytes=64, offset=6144 + 512)
+        nc.vector.tensor_copy(xo[:], xo_win[:].indirect(idx2[:]))
+        xos = reuse.tile([P, J], U8, name="xos", align_bytes=64, offset=6144 + 1536)
+        nc.vector.tensor_copy(xos[:], xos_win[:].indirect(idx2[:]))
+        w2 = reuse.tile([P, PACK, 2 * P], U8, name="w2", align_bytes=64, offset=8704)
         nc.vector.tensor_copy(w2[:].rearrange("p t (m e) -> p t m e", e=2),
                               w2_raw[:].rearrange("p (m t e) -> p t m e", t=PACK, e=2))
+        pv = []
+        for t, offset in enumerate((4096, 0, 11264, 13312)):
+            board = reuse.tile([P, C], F32, name="pv%d" % t, offset=offset)
+            nc.gpsimd.memset(board[:], 0.0)
+            pv.append(board)
         b_vals = []
         for pair in range(PACK // 2):
             acc = psum.tile([P, 2, J], F32, name="acc")
@@ -142,40 +153,43 @@ def tile_picked_tokens_plain_two_trailing_one_endsteps_kernel(
             b_vals.append(vals)
 
         g1_bufs = []
-        for e, offset in enumerate((24576, 8192)):
+        for e, offset in enumerate((6144, 8704)):
             buf = reuse.tile([P, C + 2], F32, name="g1_%d" % e, offset=offset)
             nc.vector.memset(buf[:, 0:2], 0.0)
             g1_bufs.append(buf)
         g3 = keep.tile([P, PACK, C], F32, name="g3")
         for t in range(PACK):
             g1 = g1_bufs[t % 2]
-            nc.vector.tensor_copy(g1[:, 2:3], pw[t][:, 0:1])
+            nc.vector.tensor_tensor(g1[:, 2:3], pw[t][:, 0:1], g1[:, 1:2], ADD)
             nc.vector.tensor_tensor(g1[:, 3:], pw[t][:, 1:], pw[t][:, : C - 1], ADD)
             nc.vector.tensor_tensor(g3[:, t, :], g1[:, 2:], g1[:, :C], ADD)
 
         pages = []
         for i in range(N // P):
-            page = reuse.tile([P, U], F32, name="page%d" % i, offset=16384 + 4096 * i)
+            page = reuse.tile([P, U], F32, name="page%d" % i, offset=15360 + 4096 * i)
             nc.gpsimd.memset(page[:], 0.0)
             pages.append(page)
 
-        hid = keep.tile([P, PACK - 1, C], F32, name="hid")
+        hid = keep.tile([P, PACK, C], F32, name="hid")
         for t in range(PACK):
             nc.scalar.activation(pv[t][:].indirect(idx4[:]), b_vals[t // 2][:, t % 2, :], COPY)
             if t < PACK - 1:
                 nc.vector.tensor_tensor(hid[:, t, :], g3[:, t, :], pv[t][:], MAX)
 
         last = PACK - 1
-        woven = {}
-        for c0, c1 in CHUNKS:
-            woven[c0] = keep.tile([P, c1 - c0, PACK], BF16, name="woven%d" % c0, align_bytes=64)
-            nc.vector.tensor_copy(woven[c0][:, :, :last], hid[:, :, c0:c1].rearrange("p t c -> p c t"))
         for c0, c1 in CHUNKS:
             width = c1 - c0
-            nc.vector.tensor_tensor(woven[c0][:, :, last], g3[:, last, c0:c1], pv[last][:, c0:c1], MAX)
+            woven = keep.tile([P, width, PACK], BF16, name="woven%d" % c0, align_bytes=64)
+            if c0 == 0:
+                nc.vector.tensor_copy(woven[:, :, :last], hid[:, :last, c0:c1].rearrange("p t c -> p c t"))
+                nc.vector.tensor_tensor(woven[:, :, last], g3[:, last, c0:c1], pv[last][:, c0:c1], MAX)
+            else:
+                nc.vector.tensor_tensor(hid[:, last, c0:c1], g3[:, last, c0:c1], pv[last][:, c0:c1], MAX)
+                nc.vector.tensor_copy(woven[:].rearrange("p (c i) t -> p c t i", i=4),
+                                      hid[:, :, c0:c1].rearrange("p t (c i) -> p c t i", i=4))
             codes = keep.tile([P, width], U32, name="codes%d" % c0, align_bytes=64)
             scales = keep.tile([P, width], U8, name="scales%d" % c0, align_bytes=64)
-            nc.vector.quantize_mx(codes[:].bitcast(FP8X4), scales[:], woven[c0][:].rearrange("p c t -> p (c t)"))
+            nc.vector.quantize_mx(codes[:].bitcast(FP8X4), scales[:], woven[:].rearrange("p c t -> p (c t)"))
             p_vals = keep.tile([P, N // P, width], F32, name="p%d" % c0)
 
             def product(acc, i):

from contextlib import ExitStack

import concourse.mybir as mybir

K, J, R, T, Z, M, C, N, U = 512, 256, 512, 1024, 512, 1024, 512, 256, 1024
FLOPS = 2 * (K * R * J + Z * R * J + R * N * C)

P = 128
PACK = 4
F32 = mybir.dt.float32
BF16 = mybir.dt.bfloat16
I32 = mybir.dt.int32
U32 = mybir.dt.uint32
U16 = mybir.dt.uint16
U8 = mybir.dt.uint8
FP8X4 = mybir.dt.float8_e4m3fn_x4
FP4X4 = mybir.dt.float4_e2m1fn_x4
ADD = mybir.AluOpType.add
SUB = mybir.AluOpType.subtract
MAX = mybir.AluOpType.max
COPY = mybir.ActivationFunctionType.Copy

CHUNKS = ((0, 128), (128, 256), (256, 512))
STORE_COLS = 256


def tile_picked_tokens_plain_two_trailing_one_endsteps_kernel(
    tc, xt_words, xt_scales, w_words, w_scales, xo_words, xo_scales, w2_words, w2_scales,
    wb_words, wb_scales, offs, offs2, offs3, offs4, offs5, out,
):
    nc = tc.nc
    with ExitStack() as ctx:
        lists = ctx.enter_context(tc.tile_pool(name="lists", bufs=1))
        keep = ctx.enter_context(tc.tile_pool(name="keep", bufs=1))
        reuse = ctx.enter_context(tc.tile_pool(name="reuse", bufs=1))
        psum = ctx.enter_context(tc.psum_pool(name="psum", bufs=8))

        def load_list(name, src):
            tile = lists.tile(list(src.shape), U16, name=name)
            nc.sync.dma_start(tile[:], src)
            return tile

        def zeroed_plane(name, width, engine):
            plane = keep.tile([P, width], U8, name=name, align_bytes=64)
            engine.memset(plane[:].bitcast(I32), 0)
            return plane

        def load_scales(plane, src):
            rows = src[0].bitcast(I32)
            for q in range(4):
                nc.sync.dma_start(plane[32 * q : 32 * q + 4, :].bitcast(I32), rows[4 * q : 4 * q + 4, :])

        def e4m3_words(src):
            return src[0].rearrange("p c r -> p (c r)").bitcast(I32)

        xts_win = zeroed_plane("xts_win", T, nc.vector)
        ws_raw = reuse.tile([P, R], U8, name="ws_raw", offset=23552)
        nc.vector.memset(ws_raw[:].bitcast(I32), 0)
        idx = load_list("idx", offs)
        xts_stage = keep.tile([P, 2, T // 4], I32, name="xts_stage")
        xts_rows = xt_scales[0].bitcast(I32)
        for part in range(2):
            nc.sync.dma_start(xts_stage[64 * part : 64 * part + 4, :, :],
                              xts_rows[8 * part : 8 * part + 8, :].rearrange("(q i) n -> i q n", i=4))
        w2s_stage = keep.tile([4, 4, R // 4], I32, name="w2s_stage")
        nc.sync.dma_start(w2s_stage[:], w2_scales[0].bitcast(I32).rearrange("(q i) n -> i q n", i=4))
        xt_win = reuse.tile([P, T], U32, name="xt_win", offset=0)
        nc.sync.dma_start(xt_win[:].bitcast(I32), e4m3_words(xt_words))
        w_raw = reuse.tile([P, R], U32, name="w_raw", offset=4096)
        nc.sync.dma_start(w_raw[:].bitcast(I32), e4m3_words(w_words))
        idx3 = load_list("idx3", offs3)
        idx2 = load_list("idx2", offs2)
        load_scales(ws_raw, w_scales)

        xos_win = zeroed_plane("xos_win", M, nc.gpsimd)
        wbs = zeroed_plane("wbs", N, nc.gpsimd)

        xo_win = keep.tile([P, M], U32, name="xo_win")
        nc.sync.dma_start(xo_win[:].bitcast(I32), e4m3_words(xo_words))
        w2_raw = keep.tile([P, 2 * R], U8, name="w2_raw")
        nc.sync.dma_start(w2_raw[:].bitcast(I32), w2_words[0].bitcast(I32))
        load_scales(xos_win, xo_scales)
        idx4 = load_list("idx4", offs4)
        wb = keep.tile([P, 2 * N], U8, name="wb", align_bytes=64)
        nc.sync.dma_start(wb[:].bitcast(I32), wb_words[0].bitcast(I32))
        idx5 = load_list("idx5", offs5)
        load_scales(wbs, wb_scales)

        pw = []
        for t in range(PACK):
            board = reuse.tile([P, C], F32, name="pw%d" % t, offset=15360 + 2048 * t)
            nc.gpsimd.memset(board[:], 0.0)
            pw.append(board)

        for q in range(4):
            base = 64 * (q // 2)
            nc.vector.tensor_copy(xts_win[32 * q : 32 * q + 4, :].bitcast(I32), xts_stage[base : base + 4, q % 2, :])
        half = J // 2
        xts = keep.tile([P, J], U8, name="xts", align_bytes=64)
        xt = reuse.tile([P, J], U32, name="xt", align_bytes=64, offset=8704)
        nc.vector.tensor_copy(xts[:], xts_win[:].indirect(idx[:]))
        nc.vector.tensor_copy(xt[:], xt_win[:].indirect(idx[:]))
        ws_first = reuse.tile([P, P], U8, name="ws_first", align_bytes=64, offset=0)
        ws_rest = reuse.tile([P, PACK - 1, P], U8, name="ws_rest", align_bytes=64, offset=128)
        ws_by_t = ws_raw[:].rearrange("p (m t) -> p t m", t=PACK)
        nc.vector.tensor_copy(ws_first[:], ws_by_t[:, 0, :])
        nc.vector.tensor_copy(ws_rest[:], ws_by_t[:, 1:, :])
        w_first = reuse.tile([P, P], U32, name="w_first", align_bytes=64, offset=6144)
        w_rest = reuse.tile([P, PACK - 1, P], U32, name="w_rest", align_bytes=64, offset=6656)
        w_by_m = w_raw[:].rearrange("p (m t) -> p m t", t=PACK)
        nc.scalar.copy(w_first[:], w_by_m[:, :, 0])
        nc.scalar.copy(w_rest[:].rearrange("p t m -> p m t"), w_by_m[:, :, 1:])

        a_vals = [reuse.tile([P, J], F32, name="a%d" % t, offset=11264 + 1024 * t) for t in range(PACK)]
        for step, (t, j0, j1) in enumerate(((0, 0, half), (1, 0, J), (0, half, J), (2, 0, J), (3, 0, J))):
            acc = psum.tile([P, j1 - j0], F32, name="acc")
            w_t, ws_t = (w_first[:], ws_first[:]) if t == 0 else (w_rest[:, t - 1, :], ws_rest[:, t - 1, :])
            nc.tensor.matmul_mx(acc[:], lhsT=w_t.bitcast(FP8X4), lhsT_scale=ws_t,
                                rhs=xt[:, j0:j1].bitcast(FP8X4), rhs_scale=xts[:, j0:j1], start=True, stop=True)
            if step == 0:
                nc.scalar.activation(a_vals[t][:, j0:j1], acc[:], COPY)
            else:
                nc.vector.tensor_copy(a_vals[t][:, j0:j1], acc[:])
            nc.scalar.activation(pw[t][:].indirect(idx3[:, j0 // 16 : j1 // 16]), a_vals[t][:, j0:j1], COPY)

        w2s_raw = reuse.tile([P, R], U8, name="w2s_raw", offset=23552)
        nc.vector.memset(w2s_raw[:].bitcast(I32), 0)
        for q in range(4):
            nc.vector.tensor_copy(w2s_raw[32 * q : 32 * q + 4, :].bitcast(I32), w2s_stage[:, q, :])
        w2s = keep.tile([P, PACK, P], U8, name="w2s", align_bytes=64)
        nc.vector.tensor_copy(w2s[:], w2s_raw[:].rearrange("p (m t) -> p t m", t=PACK))
        xo = reuse.tile([P, J], U32, name="xo", align_bytes=64, offset=6144 + 512)
        nc.vector.tensor_copy(xo[:], xo_win[:].indirect(idx2[:]))
        xos = reuse.tile([P, J], U8, name="xos", align_bytes=64, offset=6144 + 1536)
        nc.vector.tensor_copy(xos[:], xos_win[:].indirect(idx2[:]))
        w2 = reuse.tile([P, PACK, 2 * P], U8, name="w2", align_bytes=64, offset=8704)
        nc.vector.tensor_copy(w2[:].rearrange("p t (m e) -> p t m e", e=2),
                              w2_raw[:].rearrange("p (m t e) -> p t m e", t=PACK, e=2))
        pv = []
        for t, offset in enumerate((4096, 0, 11264, 13312)):
            board = reuse.tile([P, C], F32, name="pv%d" % t, offset=offset)
            nc.gpsimd.memset(board[:], 0.0)
            pv.append(board)
        b_vals = []
        for pair in range(PACK // 2):
            acc = psum.tile([P, 2, J], F32, name="acc")
            for e in range(2):
                t = 2 * pair + e
                nc.tensor.matmul_mx(acc[:, e, :], lhsT=w2[:, t, :].bitcast(FP4X4), lhsT_scale=w2s[:, t, :],
                                    rhs=xo[:].bitcast(FP8X4), rhs_scale=xos[:], start=True, stop=True)
            vals = keep.tile([P, 2, J], F32, name="b%d" % pair)
            nc.vector.tensor_copy(vals[:], acc[:])
            b_vals.append(vals)

        g1_bufs = []
        for e, offset in enumerate((6144, 8704)):
            buf = reuse.tile([P, C + 2], F32, name="g1_%d" % e, offset=offset)
            nc.vector.memset(buf[:, 0:2], 0.0)
            g1_bufs.append(buf)
        g3 = keep.tile([P, PACK, C], F32, name="g3")
        for t in range(PACK):
            g1 = g1_bufs[t % 2]
            nc.vector.tensor_tensor(g1[:, 2:3], pw[t][:, 0:1], g1[:, 1:2], ADD)
            nc.vector.tensor_tensor(g1[:, 3:], pw[t][:, 1:], pw[t][:, : C - 1], ADD)
            nc.vector.tensor_tensor(g3[:, t, :], g1[:, 2:], g1[:, :C], ADD)

        pages = []
        for i in range(N // P):
            page = reuse.tile([P, U], F32, name="page%d" % i, offset=15360 + 4096 * i)
            nc.gpsimd.memset(page[:], 0.0)
            pages.append(page)

        hid = keep.tile([P, PACK, C], F32, name="hid")
        for t in range(PACK):
            nc.scalar.activation(pv[t][:].indirect(idx4[:]), b_vals[t // 2][:, t % 2, :], COPY)
            if t < PACK - 1:
                nc.vector.tensor_tensor(hid[:, t, :], g3[:, t, :], pv[t][:], MAX)

        last = PACK - 1
        for c0, c1 in CHUNKS:
            width = c1 - c0
            woven = keep.tile([P, width, PACK], BF16, name="woven%d" % c0, align_bytes=64)
            if c0 == 0:
                nc.vector.tensor_copy(woven[:, :, :last], hid[:, :last, c0:c1].rearrange("p t c -> p c t"))
                nc.vector.tensor_tensor(woven[:, :, last], g3[:, last, c0:c1], pv[last][:, c0:c1], MAX)
            else:
                nc.vector.tensor_tensor(hid[:, last, c0:c1], g3[:, last, c0:c1], pv[last][:, c0:c1], MAX)
                nc.vector.tensor_copy(woven[:].rearrange("p (c i) t -> p c t i", i=4),
                                      hid[:, :, c0:c1].rearrange("p t (c i) -> p c t i", i=4))
            codes = keep.tile([P, width], U32, name="codes%d" % c0, align_bytes=64)
            scales = keep.tile([P, width], U8, name="scales%d" % c0, align_bytes=64)
            nc.vector.quantize_mx(codes[:].bitcast(FP8X4), scales[:], woven[:].rearrange("p c t -> p (c t)"))
            p_vals = keep.tile([P, N // P, width], F32, name="p%d" % c0)

            def product(acc, i):
                nc.tensor.matmul_mx(acc, lhsT=wb[:, 2 * P * i : 2 * P * (i + 1)].bitcast(FP4X4),
                                    lhsT_scale=wbs[:, P * i : P * (i + 1)],
                                    rhs=codes[:].bitcast(FP8X4), rhs_scale=scales[:], start=True, stop=True)

            if c0 == 0:
                accs = [psum.tile([P, width], F32, name="acc") for i in range(N // P)]
                for i in range(N // P):
                    product(accs[i][:], i)
                nc.scalar.activation(p_vals[:, 0, :], accs[0][:], COPY)
                nc.vector.tensor_copy(p_vals[:, 1, :], accs[1][:])
            else:
                acc = psum.tile([P, N // P, width], F32, name="acc")
                for i in range(N // P):
                    product(acc[:, i, :], i)
                nc.vector.tensor_copy(p_vals[:], acc[:])
            for i in range(N // P):
                nc.scalar.activation(pages[i][:].indirect(idx5[:, c0 // 16 : c1 // 16]), p_vals[:, i, :], COPY)

        for i in range(N // P):
            y = keep.tile([P, U], F32, name="y%d" % i)
            if i == 0:
                nc.vector.tensor_copy(y[:, 0:1], pages[i][:, 0:1])
            else:
                nc.scalar.copy(y[:, 0:1], pages[i][:, 0:1])
            for u0 in range(0, U, STORE_COLS):
                lo, hi = max(u0, 1), u0 + STORE_COLS
                nc.vector.tensor_tensor(y[:, lo:hi], pages[i][:, lo:hi], pages[i][:, lo - 1 : hi - 1], SUB)
                nc.sync.dma_start(out[P * i : P * (i + 1), u0:hi], y[:, u0:hi])
